import numpy as np
import ml_dtypes


def mxq(x, axis, fmt="e4m3"):
    dtype, down = {"e4m3": (ml_dtypes.float8_e4m3fn, 7), "e5m2": (ml_dtypes.float8_e5m2, 14)}[fmt]
    v = np.moveaxis(np.asarray(x, np.float32).astype(ml_dtypes.bfloat16).astype(np.float64), axis, -1)
    blocks = v.reshape(v.shape[:-1] + (-1, 32))
    amax = np.abs(blocks).max(-1, keepdims=True)
    byte = np.maximum(np.where(amax > 0, np.frexp(amax)[1] - 1 + 127, 0) - down, 1)
    scale = np.exp2(byte - 127.0)
    codes = (blocks / scale).astype(np.float32).astype(dtype).astype(np.float64)
    return np.moveaxis((codes * scale).reshape(v.shape), -1, axis)


WIDE = False


def mx_kscale(k):
    if not WIDE:
        return np.ones(k)
    levels = np.array([10, -10, 5, -5, 0])
    if k % 512:
        return np.exp2(np.random.permutation(np.resize(levels, k // 32))).repeat(32)
    a = np.empty((k // 512, 16))
    for p in range(k // 512):
        a[p, :8] = np.random.permutation(np.resize(levels, 8))
        for g in range(8):
            far = levels[np.abs(levels - a[p, g]) >= 10]
            a[p, g + 8] = far[np.random.randint(len(far))]
    return np.exp2(a.ravel()).repeat(32)


def f64(x):
    return np.asarray(x).astype(np.float64)


def striped(idx):
    return np.tile(idx.reshape(-1, 16).T, (8, 1)).astype(np.uint16)


def unstriped(offs):
    return offs[:16].T.reshape(-1).astype(np.int64)


def striped8(idx):
    return np.concatenate([x.reshape(-1, 16).T for x in idx]).astype(np.uint16)


def runs(offs, k):
    lists = np.stack([offs[16 * r : 16 * r + 16].T.reshape(-1) for r in range(8)]).astype(np.int64)
    return lists[np.arange(k) % 512 // 64]


def pack_weight(w):
    k, n = w.shape
    w = f64(np.asarray(w, np.float32).astype(ml_dtypes.bfloat16)).reshape(k // 32, 32, n)
    amax = np.abs(w).max(1)
    byte = np.clip(np.where(amax > 0, np.frexp(amax)[1] - 1 + 127 - 7, 1), 1, 254)
    scaled = (w * np.exp2(127.0 - byte)[:, None, :]).reshape(k, n).astype(np.float32)
    words = np.ascontiguousarray(scaled.reshape(k // 512, 128, 4, n).transpose(0, 1, 3, 2)).astype(ml_dtypes.float8_e4m3fn).view(np.uint8)
    return words, np.ascontiguousarray(byte.astype(np.uint8).reshape(k // 512, 16, n))


def unpack_weight(words, scales):
    g, p, n, _ = words.shape
    vals = np.ascontiguousarray(words).view(ml_dtypes.float8_e4m3fn).astype(np.float64) * np.repeat(np.exp2(scales.astype(np.float64) - 127.0), 8, axis=1)[..., None]
    return vals.transpose(0, 1, 3, 2).reshape(g * 512, n)


K, T, S, H, G, U = 512, 1024, 512, 512, 2048, 1024


def setup_inputs():
    n = np.random.standard_normal
    s = mx_kscale(K)[:, None]
    packed_xT = pack_weight(n((K, T)) * s)
    packed_dT = pack_weight(n((K, G)) / s)
    return {
        "x_words": packed_xT[0],
        "x_scales": packed_xT[1],
        "w1": (n((K, H)) / np.sqrt(K) / s).astype(np.float32),
        "w2": (n((K, H)) / np.sqrt(K) / s).astype(np.float32),
        "gs": (np.random.uniform(0.5, 1.5, (K, 1)) * s).astype(np.float32),
        "d_words": packed_dT[0],
        "d_scales": packed_dT[1],
        "mem": n((H, U)).astype(np.float32),
        "offs": striped(np.random.permutation(T)[:S]),
        "two": striped(np.random.permutation(T)[:S]),
        "n1": striped8(np.stack([np.random.permutation(S) for _ in range(8)])),
        "n2": striped8(np.stack([np.random.permutation(S) for _ in range(8)])),
        "n3": striped8(np.stack([np.random.permutation(S) for _ in range(8)])),
        "k1": striped8(np.random.randint(0, G, (8, H))),
        "n4": striped8(np.stack([np.random.permutation(U)[:S] for _ in range(8)])),
    }


def reference(x_words, x_scales, w1, w2, gs, d_words, d_scales, mem, offs, two, n1, n2, n3, k1, n4):
    d_k1 = unpack_weight(d_words, d_scales)[np.arange(K)[:, None], runs(k1, K)]
    xq = unpack_weight(x_words, x_scales)[:, unstriped(offs)]
    y = mxq(f64(w1), 0, "e4m3").T @ xq
    x_two = unpack_weight(x_words, x_scales)[:, unstriped(two)]
    d = mxq(f64(w2), 0, "e4m3").T @ x_two
    z = f64(gs) * (np.maximum(np.minimum(y - (0.5 * (y[np.arange(H)[:, None], runs(n1, H)])), d[np.arange(H)[:, None], runs(n2, H)]), d[np.arange(H)[:, None], runs(n3, H)]))
    h = 0.0625 * ((d_k1.T @ mxq(z, 0, "e4m3")))
    out = f64(mem).copy()
    out[np.arange(H)[:, None], runs(n4, H)] = h
    return out

@@ -1,0 +1,206 @@
+from contextlib import ExitStack
+
+import concourse.mybir as mybir
+
+K, T, S, H, G, U = 512, 1024, 512, 512, 2048, 1024
+FLOPS = 3 * 2 * 512 * 512 * 512
+
+F32 = mybir.dt.float32
+BF16 = mybir.dt.bfloat16
+I32 = mybir.dt.int32
+U32 = mybir.dt.uint32
+U16 = mybir.dt.uint16
+U8 = mybir.dt.uint8
+FP8X4 = mybir.dt.float8_e4m3fn_x4
+ALU = mybir.AluOpType
+COPY = mybir.ActivationFunctionType.Copy
+
+P = 128
+PACK = 4
+CHUNK = 256
+CHUNKS = S // CHUNK
+COLS = CHUNK // 16
+HALF = H // 2
+
+
+def tile_picked_twqclampbpage_none_p_kernel(
+    tc, x_words, x_scales, w1, w2, gs, d_words, d_scales, mem, offs, two, n1, n2, n3, k1, n4, out
+):
+    nc = tc.nc
+    with ExitStack() as ctx:
+        keep = ctx.enter_context(tc.tile_pool(name="keep", bufs=1))
+        psum = ctx.enter_context(tc.psum_pool(name="psum", bufs=8))
+
+        def load_list(src, name):
+            tile = keep.tile([P, S // 16], U16, name=name)
+            nc.sync.dma_start(tile[:], src)
+            return tile
+
+        def load_weight(src, half, name):
+            tile = keep.tile([P, PACK, HALF], F32, name=name, tag=name, align_bytes=64)
+            rows = src.rearrange("(p j) c -> p j c", j=PACK)
+            nc.sync.dma_start(tile[:], rows[:, :, half * HALF : (half + 1) * HALF])
+            return tile
+
+        def load_words(src, width, name):
+            tile = keep.tile([P, width], I32, name=name)
+            nc.sync.dma_start(tile[:], src[0].rearrange("p n r -> p (n r)").bitcast(I32))
+            return tile
+
+        x_scale_table = keep.tile([P, T], U8, name="x_scale_table")
+        nc.vector.memset(x_scale_table[:].bitcast(I32), 0)
+        d_scale_table = keep.tile([P, G], U8, name="d_scale_table")
+        nc.vector.memset(d_scale_table[:].bitcast(I32), 0)
+        d_scale_rows = keep.tile([P, H], U8, name="d_scale_rows", align_bytes=64)
+        nc.vector.memset(d_scale_rows[:].bitcast(I32), 0)
+        offs_t = load_list(offs, "offs_t")
+        two_t = load_list(two, "two_t")
+        for q in range(4):
+            nc.sync.dma_start(
+                x_scale_table[32 * q : 32 * q + 4, :].bitcast(I32), x_scales[0, 4 * q : 4 * q + 4, :].bitcast(I32)
+            )
+        x_table = load_words(x_words, T, "x_table")
+        w1_raw = [load_weight(w1, half, "w1_raw%d" % half) for half in range(2)]
+
+        k1_t = load_list(k1, "k1_t")
+        d_rows = d_scales[0].rearrange("(r e) c -> e r c", e=2)
+        for e in range(2):
+            nc.sync.dma_start(d_scale_table[e:P:16, :].bitcast(I32), d_rows[e].bitcast(I32))
+        d_table = load_words(d_words, G, "d_table")
+        w2_raw = [load_weight(w2, half, "w2_raw%d" % half) for half in range(2)]
+        n1_t = load_list(n1, "n1_t")
+        gain = keep.tile([P, PACK], F32, name="gain")
+        nc.sync.dma_start(gain[:], gs.rearrange("(p t) o -> p (t o)", t=PACK))
+        n2_t = load_list(n2, "n2_t")
+        n3_t = load_list(n3, "n3_t")
+        n4_t = load_list(n4, "n4_t")
+        mem_rows = mem.rearrange("(p t) u -> t p u", t=PACK)
+        out_rows = out.rearrange("(p t) u -> t p u", t=PACK)
+        pages = []
+        for t in range(PACK):
+            page = keep.tile([P, U], F32, name="page%d" % t)
+            nc.sync.dma_start(page[:], mem_rows[t])
+            pages.append(page)
+
+        def gather_packed(table, offsets, dtype, name, tag):
+            picked = keep.tile([P, S], dtype, name=name, tag=tag, align_bytes=64)
+            nc.vector.tensor_copy(picked[:], table.indirect(offsets[:]))
+            return picked
+
+        def cast_weight(grouped, raw, half):
+            m_half = HALF // PACK
+            nc.scalar.copy(
+                grouped[:, :, half * m_half : (half + 1) * m_half, :].rearrange("p t m j -> p m j t"),
+                raw[half][:].rearrange("p j (m t) -> p m j t", t=PACK),
+            )
+
+        def quantize(values, width, name, tag):
+            codes = keep.tile([P, width], U32, name=name + "_codes", tag=tag, align_bytes=64)
+            scales = keep.tile([P, width], U8, name=name + "_scales", align_bytes=64)
+            nc.vector.quantize_mx(out=codes[:].bitcast(FP8X4), scales=scales[:], in_=values)
+            return codes, scales
+
+        def product(lhs_codes, lhs_scales, t, rhs_codes, rhs_scales, width):
+            acc = psum.tile([P, width], F32, name="acc")
+            cols = slice(t * P, (t + 1) * P)
+            nc.tensor.matmul_mx(
+                out=acc[:],
+                lhsT=lhs_codes[:, cols].bitcast(FP8X4),
+                lhsT_scale=lhs_scales[:, cols],
+                rhs=rhs_codes[:].bitcast(FP8X4),
+                rhs_scale=rhs_scales[:],
+                start=True,
+                stop=True,
+            )
+            return acc
+
+        xa_scales = gather_packed(x_scale_table[:], offs_t, U8, "xa_scales", "xa_scales")
+        xb_scales = gather_packed(x_scale_table[:], two_t, U8, "xb_scales", "xb_scales")
+        xa_words = gather_packed(x_table[:].bitcast(U32), offs_t, U32, "xa_words", "xa_words")
+        xb_words = gather_packed(x_table[:].bitcast(U32), two_t, U32, "xb_words", "xb_words")
+
+        w1_bf = keep.tile([P, PACK, P, PACK], BF16, name="w1_bf", tag="w1_bf", align_bytes=64)
+        w2_bf = keep.tile([P, PACK, P, PACK], BF16, name="w2_bf", tag="w2_bf", align_bytes=64)
+        cast_weight(w1_bf, w1_raw, 0)
+        cast_weight(w1_bf, w1_raw, 1)
+        w1_codes, w1_scales = quantize(w1_bf[:].rearrange("p t m j -> p (t m j)"), H, "w1", "w1_codes")
+        picked_scales = gather_packed(d_scale_table[:], k1_t, U8, "picked_scales", "w1_bf")
+        dealt_scales = keep.tile([P, PACK, P], U8, name="dealt_scales")
+        nc.vector.tensor_copy(
+            dealt_scales[:].rearrange("p t m -> p m t"), picked_scales[:].rearrange("p (m t) -> p m t", t=PACK)
+        )
+        dealt_flat = dealt_scales[:].rearrange("p t m -> p (t m)").bitcast(I32)
+        for i in range(4):
+            first = 16 * (i // 2) + i % 2
+            nc.sync.dma_start(d_scale_rows[i:P:32, :].bitcast(I32), dealt_flat[first:P:32, :])
+
+        picked_words = gather_packed(d_table[:].bitcast(U32), k1_t, U32, "picked_words", "picked_words")
+        d_codes = keep.tile([P, H], U32, name="d_codes", align_bytes=64)
+        nc.vector.tensor_copy(
+            d_codes[:].rearrange("p (t m) -> p m t", t=PACK), picked_words[:].rearrange("p (m t) -> p m t", t=PACK)
+        )
+
+        y, half_y = [], []
+        for t in range(PACK):
+            if t == PACK - 1:
+                cast_weight(w2_bf, w2_raw, 0)
+                cast_weight(w2_bf, w2_raw, 1)
+                w2_codes, w2_scales = quantize(w2_bf[:].rearrange("p t m j -> p (t m j)"), H, "w2", "w2_codes")
+            acc = product(w1_codes, w1_scales, t, xa_words, xa_scales, S)
+            half_t = keep.tile([P, S], F32, name="half_y%d" % t)
+            nc.scalar.activation(half_t[:], acc[:], COPY, scale=-0.5)
+            y_t = keep.tile([P, S], F32, name="y%d" % t)
+            nc.scalar.copy(y_t[:], acc[:])
+            y.append(y_t)
+            half_y.append(half_t)
+
+        d = []
+        for t in range(PACK):
+            acc = product(w2_codes, w2_scales, t, xb_words, xb_scales, S)
+            d_t = keep.tile([P, S], F32, name="d%d" % t)
+            nc.scalar.copy(d_t[:], acc[:])
+            d.append(d_t)
+
+        lows = []
+        for c in range(CHUNKS):
+            low = keep.tile([P, PACK, CHUNK], F32, name="a%d" % c)
+            for t in range(PACK):
+                nc.vector.tensor_tensor(
+                    low[:, t, :],
+                    half_y[t][:].indirect(n1_t[:, c * COLS : (c + 1) * COLS]),
+                    y[t][:, c * CHUNK : (c + 1) * CHUNK],
+                    ALU.add,
+                )
+            lows.append(low)
+
+        z_bf = []
+        for c in range(CHUNKS):
+            second = keep.tile([P, PACK, CHUNK], F32, name="second%d" % c, tag="second")
+            third = keep.tile([P, PACK, CHUNK], F32, name="third%d" % c, tag="third")
+            for t in range(PACK):
+                nc.vector.tensor_copy(second[:, t, :], d[t][:].indirect(n2_t[:, c * COLS : (c + 1) * COLS]))
+            least = keep.tile([P, PACK, CHUNK], F32, name="least%d" % c)
+            for t in range(PACK):
+                nc.vector.tensor_copy(third[:, t, :], d[t][:].indirect(n3_t[:, c * COLS : (c + 1) * COLS]))
+                if t == 0:
+                    nc.vector.tensor_tensor(least[:], lows[c][:], second[:], ALU.min)
+            clamp = keep.tile([P, PACK, CHUNK], F32, name="clamp%d" % c, tag="woven%d" % (c - 1), align_bytes=64)
+            nc.vector.tensor_tensor(clamp[:], least[:], third[:], ALU.max)
+            planes = keep.tile([P, PACK, CHUNK], BF16, name="planes%d" % c, tag="planes%d" % c)
+            for t in range(PACK):
+                nc.scalar.activation(planes[:, t, :], clamp[:, t, :], COPY, scale=gain[:, t : t + 1])
+            woven = keep.tile([P, CHUNK, PACK], BF16, name="woven%d" % c, tag="woven%d" % c, align_bytes=64)
+            nc.scalar.copy(
+                woven[:].rearrange("p (c i) t -> p c t i", i=4), planes[:].rearrange("p t (c i) -> p c t i", i=4)
+            )
+            z_bf.append(quantize(woven[:].rearrange("p c t -> p (c t)"), CHUNK, "z%d" % c, "z_codes%d" % c))
+
+        for c in range(CHUNKS):
+            z_codes, z_scales = z_bf[c]
+            for t in range(PACK):
+                acc = product(d_codes, d_scale_rows, t, z_codes, z_scales, CHUNK)
+                h = keep.tile([P, CHUNK], F32, name="h%d_%d" % (c, t), tag="planes1" if (c, t) == (0, 2) else "h%d_%d" % (c, t))
+                nc.scalar.activation(h[:], acc[:], COPY, scale=0.0625)
+                nc.vector.tensor_copy(pages[t][:].indirect(n4_t[:, c * COLS : (c + 1) * COLS]), h[:])
+                if c == CHUNKS - 1:
+                    nc.sync.dma_start(out_rows[t], pages[t][:])

@@ -14,6 +14,8 @@ U8 = mybir.dt.uint8
 FP8X4 = mybir.dt.float8_e4m3fn_x4
 ALU = mybir.AluOpType
 COPY = mybir.ActivationFunctionType.Copy
+ABS = mybir.ActivationFunctionType.Abs
+SIGN = mybir.ActivationFunctionType.Sign
 
 P = 128
 PACK = 4
@@ -53,6 +55,9 @@ def tile_picked_twqclampbpage_none_p_kernel(
         nc.vector.memset(d_scale_table[:].bitcast(I32), 0)
         d_scale_rows = keep.tile([P, H], U8, name="d_scale_rows", align_bytes=64)
         nc.vector.memset(d_scale_rows[:].bitcast(I32), 0)
+        windows = [keep.tile([P, 2 * S], F32, name="half_y%d" % t) for t in range(PACK)]
+        nc.vector.memset(windows[0][:, S:], 0.0)
+        last_y = keep.tile([P, S], F32, name="last_y")
         offs_t = load_list(offs, "offs_t")
         two_t = load_list(two, "two_t")
         for q in range(4):
@@ -66,11 +71,11 @@ def tile_picked_twqclampbpage_none_p_kernel(
         d_rows = d_scales[0].rearrange("(r e) c -> e r c", e=2)
         for e in range(2):
             nc.sync.dma_start(d_scale_table[e:P:16, :].bitcast(I32), d_rows[e].bitcast(I32))
+        gain = keep.tile([P, PACK], F32, name="gain")
+        nc.sync.dma_start(gain[:], gs.rearrange("(p t) o -> p (t o)", t=PACK))
         d_table = load_words(d_words, G, "d_table")
         w2_raw = [load_weight(w2, half, "w2_raw%d" % half) for half in range(2)]
         n1_t = load_list(n1, "n1_t")
-        gain = keep.tile([P, PACK], F32, name="gain")
-        nc.sync.dma_start(gain[:], gs.rearrange("(p t) o -> p (t o)", t=PACK))
         n2_t = load_list(n2, "n2_t")
         n3_t = load_list(n3, "n3_t")
         n4_t = load_list(n4, "n4_t")
@@ -123,72 +128,73 @@ def tile_picked_twqclampbpage_none_p_kernel(
         w2_bf = keep.tile([P, PACK, P, PACK], BF16, name="w2_bf", tag="w2_bf", align_bytes=64)
         cast_weight(w1_bf, w1_raw, 0)
         cast_weight(w1_bf, w1_raw, 1)
+        size = keep.tile([P, PACK], F32, name="size")
+        nc.scalar.activation(size[:], gain[:], ABS)
+        half_size = keep.tile([P, PACK], F32, name="half_size")
+        nc.scalar.activation(half_size[:], size[:], COPY, scale=-0.5)
+        sign = keep.tile([P, PACK], F32, name="sign")
+        nc.scalar.activation(sign[:], gain[:], SIGN)
         w1_codes, w1_scales = quantize(w1_bf[:].rearrange("p t m j -> p (t m j)"), H, "w1", "w1_codes")
         picked_scales = gather_packed(d_scale_table[:], k1_t, U8, "picked_scales", "w1_bf")
         dealt_scales = keep.tile([P, PACK, P], U8, name="dealt_scales")
         nc.vector.tensor_copy(
-            dealt_scales[:].rearrange("p t m -> p m t"), picked_scales[:].rearrange("p (m t) -> p m t", t=PACK)
+            dealt_scales[:].rearrange("p t (c i) -> p c t i", i=16),
+            picked_scales[:].rearrange("p (c i t) -> p c t i", i=16, t=PACK),
         )
         dealt_flat = dealt_scales[:].rearrange("p t m -> p (t m)").bitcast(I32)
         for i in range(4):
-            first = 16 * (i // 2) + i % 2
-            nc.sync.dma_start(d_scale_rows[i:P:32, :].bitcast(I32), dealt_flat[first:P:32, :])
+            source = 16 * (i // 2) + i % 2
+            nc.sync.dma_start(d_scale_rows[i:P:32, :].bitcast(I32), dealt_flat[source:P:32, :])
 
         picked_words = gather_packed(d_table[:].bitcast(U32), k1_t, U32, "picked_words", "picked_words")
         d_codes = keep.tile([P, H], U32, name="d_codes", align_bytes=64)
         nc.vector.tensor_copy(
-            d_codes[:].rearrange("p (t m) -> p m t", t=PACK), picked_words[:].rearrange("p (m t) -> p m t", t=PACK)
+            d_codes[:].rearrange("p (t c i) -> p c t i", i=4, t=PACK),
+            picked_words[:].rearrange("p (c i t) -> p c t i", i=4, t=PACK),
         )
 
-        y, half_y = [], []
+        y = [windows[t][:, S:] for t in range(1, PACK)] + [last_y[:]]
         for t in range(PACK):
             if t == PACK - 1:
                 cast_weight(w2_bf, w2_raw, 0)
                 cast_weight(w2_bf, w2_raw, 1)
                 w2_codes, w2_scales = quantize(w2_bf[:].rearrange("p t m j -> p (t m j)"), H, "w2", "w2_codes")
             acc = product(w1_codes, w1_scales, t, xa_words, xa_scales, S)
-            half_t = keep.tile([P, S], F32, name="half_y%d" % t)
-            nc.scalar.activation(half_t[:], acc[:], COPY, scale=-0.5)
-            y_t = keep.tile([P, S], F32, name="y%d" % t)
-            nc.scalar.copy(y_t[:], acc[:])
-            y.append(y_t)
-            half_y.append(half_t)
+            nc.scalar.activation(windows[t][:, :S], acc[:], COPY, scale=half_size[:, t : t + 1])
+            nc.scalar.activation(y[t], acc[:], COPY, scale=size[:, t : t + 1])
 
         d = []
         for t in range(PACK):
             acc = product(w2_codes, w2_scales, t, xb_words, xb_scales, S)
             d_t = keep.tile([P, S], F32, name="d%d" % t)
-            nc.scalar.copy(d_t[:], acc[:])
+            nc.scalar.activation(d_t[:], acc[:], COPY, scale=size[:, t : t + 1])
             d.append(d_t)
 
+        first = keep.tile([P, PACK, S], F32, name="first")
+        for t in range(PACK):
+            nc.vector.tensor_tensor(first[:, t, :], windows[t][:].indirect(n1_t[:]), y[t], ALU.add)
         lows = []
         for c in range(CHUNKS):
-            low = keep.tile([P, PACK, CHUNK], F32, name="a%d" % c)
-            for t in range(PACK):
-                nc.vector.tensor_tensor(
-                    low[:, t, :],
-                    half_y[t][:].indirect(n1_t[:, c * COLS : (c + 1) * COLS]),
-                    y[t][:, c * CHUNK : (c + 1) * CHUNK],
-                    ALU.add,
-                )
+            low = keep.tile([P, PACK, CHUNK], BF16, name="first%d" % c)
+            nc.scalar.copy(low[:], first[:, :, c * CHUNK : (c + 1) * CHUNK])
             lows.append(low)
 
         z_bf = []
         for c in range(CHUNKS):
-            second = keep.tile([P, PACK, CHUNK], F32, name="second%d" % c, tag="second")
-            third = keep.tile([P, PACK, CHUNK], F32, name="third%d" % c, tag="third")
+            second = keep.tile([P, PACK, CHUNK], BF16, name="second%d" % c, tag="second")
+            third = keep.tile([P, PACK, CHUNK], BF16, name="third%d" % c, tag="third")
             for t in range(PACK):
                 nc.vector.tensor_copy(second[:, t, :], d[t][:].indirect(n2_t[:, c * COLS : (c + 1) * COLS]))
-            least = keep.tile([P, PACK, CHUNK], F32, name="least%d" % c)
+            least = keep.tile([P, PACK, CHUNK], BF16, name="least%d" % c, tag="woven%d" % (c - 1), align_bytes=64)
             for t in range(PACK):
                 nc.vector.tensor_copy(third[:, t, :], d[t][:].indirect(n3_t[:, c * COLS : (c + 1) * COLS]))
                 if t == 0:
                     nc.vector.tensor_tensor(least[:], lows[c][:], second[:], ALU.min)
-            clamp = keep.tile([P, PACK, CHUNK], F32, name="clamp%d" % c, tag="woven%d" % (c - 1), align_bytes=64)
+            clamp = keep.tile([P, PACK, CHUNK], BF16, name="clamp%d" % c)
             nc.vector.tensor_tensor(clamp[:], least[:], third[:], ALU.max)
             planes = keep.tile([P, PACK, CHUNK], BF16, name="planes%d" % c, tag="planes%d" % c)
             for t in range(PACK):
-                nc.scalar.activation(planes[:, t, :], clamp[:, t, :], COPY, scale=gain[:, t : t + 1])
+                nc.scalar.activation(planes[:, t, :], clamp[:, t, :], COPY, scale=sign[:, t : t + 1])
             woven = keep.tile([P, CHUNK, PACK], BF16, name="woven%d" % c, tag="woven%d" % c, align_bytes=64)
             nc.scalar.copy(
                 woven[:].rearrange("p (c i) t -> p c t i", i=4), planes[:].rearrange("p t (c i) -> p c t i", i=4)

@@ -1,6 +1,7 @@
 from contextlib import ExitStack
 
 import concourse.mybir as mybir
+from concourse.masks import make_identity
 
 K, T, S, H, G, U = 512, 1024, 512, 512, 2048, 1024
 FLOPS = 3 * 2 * 512 * 512 * 512
@@ -23,6 +24,7 @@ CHUNK = 256
 CHUNKS = S // CHUNK
 COLS = CHUNK // 16
 HALF = H // 2
+BLOCKS = S // P
 
 
 def tile_picked_twqclampbpage_none_p_kernel(
@@ -31,7 +33,7 @@ def tile_picked_twqclampbpage_none_p_kernel(
     nc = tc.nc
     with ExitStack() as ctx:
         keep = ctx.enter_context(tc.tile_pool(name="keep", bufs=1))
-        psum = ctx.enter_context(tc.psum_pool(name="psum", bufs=8))
+        psum = ctx.enter_context(tc.psum_pool(name="psum", bufs=1))
 
         def load_list(src, name):
             tile = keep.tile([P, S // 16], U16, name=name)
@@ -55,9 +57,10 @@ def tile_picked_twqclampbpage_none_p_kernel(
         nc.vector.memset(d_scale_table[:].bitcast(I32), 0)
         d_scale_rows = keep.tile([P, H], U8, name="d_scale_rows", align_bytes=64)
         nc.vector.memset(d_scale_rows[:].bitcast(I32), 0)
-        windows = [keep.tile([P, 2 * S], F32, name="half_y%d" % t) for t in range(PACK)]
-        nc.vector.memset(windows[0][:, S:], 0.0)
-        last_y = keep.tile([P, S], F32, name="last_y")
+        ident_f32 = keep.tile([P, P], F32, name="ident_f32")
+        make_identity(nc, ident_f32[:])
+        ident_bf16 = keep.tile([P, P], BF16, name="ident_bf16")
+        make_identity(nc, ident_bf16[:])
         offs_t = load_list(offs, "offs_t")
         two_t = load_list(two, "two_t")
         for q in range(4):
@@ -74,7 +77,8 @@ def tile_picked_twqclampbpage_none_p_kernel(
         gain = keep.tile([P, PACK], F32, name="gain")
         nc.sync.dma_start(gain[:], gs.rearrange("(p t) o -> p (t o)", t=PACK))
         d_table = load_words(d_words, G, "d_table")
-        w2_raw = [load_weight(w2, half, "w2_raw%d" % half) for half in range(2)]
+        w2_raw = keep.tile([P, PACK, H], F32, name="w2_raw", tag="w2_raw")
+        nc.sync.dma_start(w2_raw[:], w2.rearrange("(p j) c -> p j c", j=PACK))
         n1_t = load_list(n1, "n1_t")
         n2_t = load_list(n2, "n2_t")
         n3_t = load_list(n3, "n3_t")
@@ -92,12 +96,8 @@ def tile_picked_twqclampbpage_none_p_kernel(
             nc.vector.tensor_copy(picked[:], table.indirect(offsets[:]))
             return picked
 
-        def cast_weight(grouped, raw, half):
-            m_half = HALF // PACK
-            nc.scalar.copy(
-                grouped[:, :, half * m_half : (half + 1) * m_half, :].rearrange("p t m j -> p m j t"),
-                raw[half][:].rearrange("p j (m t) -> p m j t", t=PACK),
-            )
+        def cast_weight(grouped, raw):
+            nc.scalar.copy(grouped.rearrange("p t m j -> p m j t"), raw.rearrange("p j (m t) -> p m j t", t=PACK))
 
         def quantize(values, width, name, tag):
             codes = keep.tile([P, width], U32, name=name + "_codes", tag=tag, align_bytes=64)
@@ -105,8 +105,8 @@ def tile_picked_twqclampbpage_none_p_kernel(
             nc.vector.quantize_mx(out=codes[:].bitcast(FP8X4), scales=scales[:], in_=values)
             return codes, scales
 
-        def product(lhs_codes, lhs_scales, t, rhs_codes, rhs_scales, width):
-            acc = psum.tile([P, width], F32, name="acc")
+        def product(lhs_codes, lhs_scales, t, rhs_codes, rhs_scales, width, bank):
+            acc = psum.tile([P, width], F32, name="acc", tag="bank%d" % bank)
             cols = slice(t * P, (t + 1) * P)
             nc.tensor.matmul_mx(
                 out=acc[:],
@@ -126,16 +126,13 @@ def tile_picked_twqclampbpage_none_p_kernel(
 
         w1_bf = keep.tile([P, PACK, P, PACK], BF16, name="w1_bf", tag="w1_bf", align_bytes=64)
         w2_bf = keep.tile([P, PACK, P, PACK], BF16, name="w2_bf", tag="w2_bf", align_bytes=64)
-        cast_weight(w1_bf, w1_raw, 0)
-        cast_weight(w1_bf, w1_raw, 1)
+        for half in range(2):
+            cast_weight(w1_bf[:, :, half * P // 2 : (half + 1) * P // 2, :], w1_raw[half][:])
         size = keep.tile([P, PACK], F32, name="size")
         nc.scalar.activation(size[:], gain[:], ABS)
-        half_size = keep.tile([P, PACK], F32, name="half_size")
-        nc.scalar.activation(half_size[:], size[:], COPY, scale=-0.5)
         sign = keep.tile([P, PACK], F32, name="sign")
         nc.scalar.activation(sign[:], gain[:], SIGN)
-        w1_codes, w1_scales = quantize(w1_bf[:].rearrange("p t m j -> p (t m j)"), H, "w1", "w1_codes")
-        picked_scales = gather_packed(d_scale_table[:], k1_t, U8, "picked_scales", "w1_bf")
+        picked_scales = gather_packed(d_scale_table[:], k1_t, U8, "picked_scales", "picked_scales")
         dealt_scales = keep.tile([P, PACK, P], U8, name="dealt_scales")
         nc.vector.tensor_copy(
             dealt_scales[:].rearrange("p t (c i) -> p c t i", i=16),
@@ -146,41 +143,67 @@ def tile_picked_twqclampbpage_none_p_kernel(
             source = 16 * (i // 2) + i % 2
             nc.sync.dma_start(d_scale_rows[i:P:32, :].bitcast(I32), dealt_flat[source:P:32, :])
 
-        picked_words = gather_packed(d_table[:].bitcast(U32), k1_t, U32, "picked_words", "picked_words")
+        w1_codes, w1_scales = quantize(w1_bf[:].rearrange("p t m j -> p (t m j)"), H, "w1", "w1_codes")
+        picked_words = gather_packed(d_table[:].bitcast(U32), k1_t, U32, "picked_words", "w1_bf")
         d_codes = keep.tile([P, H], U32, name="d_codes", align_bytes=64)
         nc.vector.tensor_copy(
             d_codes[:].rearrange("p (t c i) -> p c t i", i=4, t=PACK),
             picked_words[:].rearrange("p (c i t) -> p c t i", i=4, t=PACK),
         )
 
-        y = [windows[t][:, S:] for t in range(1, PACK)] + [last_y[:]]
+        y = []
         for t in range(PACK):
-            if t == PACK - 1:
-                cast_weight(w2_bf, w2_raw, 0)
-                cast_weight(w2_bf, w2_raw, 1)
+            if t == 2:
+                cast_weight(w2_bf[:], w2_raw[:])
                 w2_codes, w2_scales = quantize(w2_bf[:].rearrange("p t m j -> p (t m j)"), H, "w2", "w2_codes")
-            acc = product(w1_codes, w1_scales, t, xa_words, xa_scales, S)
-            nc.scalar.activation(windows[t][:, :S], acc[:], COPY, scale=half_size[:, t : t + 1])
-            nc.scalar.activation(y[t], acc[:], COPY, scale=size[:, t : t + 1])
+            acc = product(w1_codes, w1_scales, t, xa_words, xa_scales, S, t)
+            y_t = keep.tile([P, S], F32, name="y%d" % t, tag="w2_raw" if t == 2 else "y%d" % t)
+            nc.scalar.activation(y_t[:], acc[:], COPY, scale=size[:, t : t + 1])
+            y.append(y_t)
 
         d = []
         for t in range(PACK):
-            acc = product(w2_codes, w2_scales, t, xb_words, xb_scales, S)
+            acc = product(w2_codes, w2_scales, t, xb_words, xb_scales, S, PACK + t)
             d_t = keep.tile([P, S], F32, name="d%d" % t)
             nc.scalar.activation(d_t[:], acc[:], COPY, scale=size[:, t : t + 1])
             d.append(d_t)
 
-        first = keep.tile([P, PACK, S], F32, name="first")
+        sums = []
         for t in range(PACK):
-            nc.vector.tensor_tensor(first[:, t, :], windows[t][:].indirect(n1_t[:]), y[t], ALU.add)
-        lows = []
-        for c in range(CHUNKS):
-            low = keep.tile([P, PACK, CHUNK], BF16, name="first%d" % c)
-            nc.scalar.copy(low[:], first[:, :, c * CHUNK : (c + 1) * CHUNK])
-            lows.append(low)
+            total = psum.tile([P, S], F32, name="total", tag="bank%d" % t)
+            for b in range(BLOCKS):
+                cols = slice(b * P, (b + 1) * P)
+                nc.tensor.matmul(
+                    total[:, cols], y[t][:, cols], ident_f32[:], start=(b == 0), stop=False, is_transpose=True
+                )
+            sums.append(total)
+        lows = [psum.tile([P, PACK, CHUNK], BF16, name="back", tag="bank%d" % (PACK + c)) for c in range(CHUNKS)]
+        for t in range(PACK):
+            half = keep.tile([P, S], F32, name="half%d" % t)
+            for c in range(CHUNKS):
+                nc.vector.tensor_scalar(
+                    half[:, c * CHUNK : (c + 1) * CHUNK],
+                    y[t][:].indirect(n1_t[:, c * COLS : (c + 1) * COLS]),
+                    -0.5,
+                    0.0,
+                    ALU.mult,
+                    ALU.add,
+                )
+            for b in range(BLOCKS):
+                cols = slice(b * P, (b + 1) * P)
+                nc.tensor.matmul(
+                    sums[t][:, cols], half[:, cols], ident_f32[:], start=False, stop=(b == BLOCKS - 1), is_transpose=True
+                )
+            turned = keep.tile([P, S], BF16, name="turned%d" % t)
+            nc.scalar.copy(turned[:], sums[t][:])
+            for b in range(BLOCKS):
+                c, inner = divmod(b * P, CHUNK)
+                nc.tensor.transpose(lows[c][:, t, inner : inner + P], turned[:, b * P : (b + 1) * P], ident_bf16[:])
 
         z_bf = []
         for c in range(CHUNKS):
+            first = keep.tile([P, PACK, CHUNK], BF16, name="first%d" % c)
+            nc.scalar.copy(first[:], lows[c][:])
             second = keep.tile([P, PACK, CHUNK], BF16, name="second%d" % c, tag="second")
             third = keep.tile([P, PACK, CHUNK], BF16, name="third%d" % c, tag="third")
             for t in range(PACK):
@@ -189,7 +212,7 @@ def tile_picked_twqclampbpage_none_p_kernel(
             for t in range(PACK):
                 nc.vector.tensor_copy(third[:, t, :], d[t][:].indirect(n3_t[:, c * COLS : (c + 1) * COLS]))
                 if t == 0:
-                    nc.vector.tensor_tensor(least[:], lows[c][:], second[:], ALU.min)
+                    nc.vector.tensor_tensor(least[:], first[:], second[:], ALU.min)
             clamp = keep.tile([P, PACK, CHUNK], BF16, name="clamp%d" % c)
             nc.vector.tensor_tensor(clamp[:], least[:], third[:], ALU.max)
             planes = keep.tile([P, PACK, CHUNK], BF16, name="planes%d" % c, tag="planes%d" % c)
@@ -204,7 +227,7 @@ def tile_picked_twqclampbpage_none_p_kernel(
         for c in range(CHUNKS):
             z_codes, z_scales = z_bf[c]
             for t in range(PACK):
-                acc = product(d_codes, d_scale_rows, t, z_codes, z_scales, CHUNK)
+                acc = product(d_codes, d_scale_rows, t, z_codes, z_scales, CHUNK, (c * 6 + t) % 8 if c == 0 or t < 2 else t + 2)
                 h = keep.tile([P, CHUNK], F32, name="h%d_%d" % (c, t), tag="planes1" if (c, t) == (0, 2) else "h%d_%d" % (c, t))
                 nc.scalar.activation(h[:], acc[:], COPY, scale=0.0625)
                 nc.vector.tensor_copy(pages[t][:].indirect(n4_t[:, c * COLS : (c + 1) * COLS]), h[:])

from contextlib import ExitStack

import concourse.mybir as mybir
from concourse.masks import make_identity

K, T, S, H, G, U = 512, 1024, 512, 512, 2048, 1024
FLOPS = 3 * 2 * 512 * 512 * 512

F32 = mybir.dt.float32
BF16 = mybir.dt.bfloat16
I32 = mybir.dt.int32
U32 = mybir.dt.uint32
U16 = mybir.dt.uint16
U8 = mybir.dt.uint8
FP8X4 = mybir.dt.float8_e4m3fn_x4
ALU = mybir.AluOpType
COPY = mybir.ActivationFunctionType.Copy
ABS = mybir.ActivationFunctionType.Abs
SIGN = mybir.ActivationFunctionType.Sign

P = 128
PACK = 4
CHUNK = 256
CHUNKS = S // CHUNK
COLS = CHUNK // 16
HALF = H // 2
BLOCKS = S // P


def tile_picked_twqclampbpage_none_p_kernel(
    tc, x_words, x_scales, w1, w2, gs, d_words, d_scales, mem, offs, two, n1, n2, n3, k1, n4, out
):
    nc = tc.nc
    with ExitStack() as ctx:
        keep = ctx.enter_context(tc.tile_pool(name="keep", bufs=1))
        psum = ctx.enter_context(tc.psum_pool(name="psum", bufs=1))

        def load_list(src, name):
            tile = keep.tile([P, S // 16], U16, name=name)
            nc.sync.dma_start(tile[:], src)
            return tile

        def load_weight(src, half, name):
            tile = keep.tile([P, PACK, HALF], F32, name=name, tag=name, align_bytes=64)
            rows = src.rearrange("(p j) c -> p j c", j=PACK)
            nc.sync.dma_start(tile[:], rows[:, :, half * HALF : (half + 1) * HALF])
            return tile

        def load_words(src, width, name):
            tile = keep.tile([P, width], I32, name=name)
            nc.sync.dma_start(tile[:], src[0].rearrange("p n r -> p (n r)").bitcast(I32))
            return tile

        x_scale_table = keep.tile([P, T], U8, name="x_scale_table")
        nc.vector.memset(x_scale_table[:].bitcast(I32), 0)
        d_scale_table = keep.tile([P, G], U8, name="d_scale_table")
        nc.vector.memset(d_scale_table[:].bitcast(I32), 0)
        d_scale_rows = keep.tile([P, H], U8, name="d_scale_rows", align_bytes=64)
        nc.vector.memset(d_scale_rows[:].bitcast(I32), 0)
        ident_f32 = keep.tile([P, P], F32, name="ident_f32")
        make_identity(nc, ident_f32[:])
        ident_bf16 = keep.tile([P, P], BF16, name="ident_bf16")
        make_identity(nc, ident_bf16[:])
        offs_t = load_list(offs, "offs_t")
        two_t = load_list(two, "two_t")
        for q in range(4):
            nc.sync.dma_start(
                x_scale_table[32 * q : 32 * q + 4, :].bitcast(I32), x_scales[0, 4 * q : 4 * q + 4, :].bitcast(I32)
            )
        x_table = load_words(x_words, T, "x_table")
        w1_raw = [load_weight(w1, half, "w1_raw%d" % half) for half in range(2)]

        k1_t = load_list(k1, "k1_t")
        d_rows = d_scales[0].rearrange("(r e) c -> e r c", e=2)
        for e in range(2):
            nc.sync.dma_start(d_scale_table[e:P:16, :].bitcast(I32), d_rows[e].bitcast(I32))
        gain = keep.tile([P, PACK], F32, name="gain")
        nc.sync.dma_start(gain[:], gs.rearrange("(p t) o -> p (t o)", t=PACK))
        d_table = load_words(d_words, G, "d_table")
        w2_raw = keep.tile([P, PACK, H], F32, name="w2_raw", tag="w2_raw")
        nc.sync.dma_start(w2_raw[:], w2.rearrange("(p j) c -> p j c", j=PACK))
        n1_t = load_list(n1, "n1_t")
        n2_t = load_list(n2, "n2_t")
        n3_t = load_list(n3, "n3_t")
        n4_t = load_list(n4, "n4_t")
        mem_rows = mem.rearrange("(p t) u -> t p u", t=PACK)
        out_rows = out.rearrange("(p t) u -> t p u", t=PACK)
        pages = []
        for t in range(PACK):
            page = keep.tile([P, U], F32, name="page%d" % t)
            nc.sync.dma_start(page[:], mem_rows[t])
            pages.append(page)

        def gather_packed(table, offsets, dtype, name, tag):
            picked = keep.tile([P, S], dtype, name=name, tag=tag, align_bytes=64)
            nc.vector.tensor_copy(picked[:], table.indirect(offsets[:]))
            return picked

        def cast_weight(grouped, raw):
            nc.scalar.copy(grouped.rearrange("p t m j -> p m j t"), raw.rearrange("p j (m t) -> p m j t", t=PACK))

        def quantize(values, width, name, tag):
            codes = keep.tile([P, width], U32, name=name + "_codes", tag=tag, align_bytes=64)
            scales = keep.tile([P, width], U8, name=name + "_scales", align_bytes=64)
            nc.vector.quantize_mx(out=codes[:].bitcast(FP8X4), scales=scales[:], in_=values)
            return codes, scales

        def product(lhs_codes, lhs_scales, t, rhs_codes, rhs_scales, width, bank):
            acc = psum.tile([P, width], F32, name="acc", tag="bank%d" % bank)
            cols = slice(t * P, (t + 1) * P)
            nc.tensor.matmul_mx(
                out=acc[:],
                lhsT=lhs_codes[:, cols].bitcast(FP8X4),
                lhsT_scale=lhs_scales[:, cols],
                rhs=rhs_codes[:].bitcast(FP8X4),
                rhs_scale=rhs_scales[:],
                start=True,
                stop=True,
            )
            return acc

        xa_scales = gather_packed(x_scale_table[:], offs_t, U8, "xa_scales", "xa_scales")
        xb_scales = gather_packed(x_scale_table[:], two_t, U8, "xb_scales", "xb_scales")
        xa_words = gather_packed(x_table[:].bitcast(U32), offs_t, U32, "xa_words", "xa_words")
        xb_words = gather_packed(x_table[:].bitcast(U32), two_t, U32, "xb_words", "xb_words")

        w1_bf = keep.tile([P, PACK, P, PACK], BF16, name="w1_bf", tag="w1_bf", align_bytes=64)
        w2_bf = keep.tile([P, PACK, P, PACK], BF16, name="w2_bf", tag="w2_bf", align_bytes=64)
        for half in range(2):
            cast_weight(w1_bf[:, :, half * P // 2 : (half + 1) * P // 2, :], w1_raw[half][:])
        size = keep.tile([P, PACK], F32, name="size")
        nc.scalar.activation(size[:], gain[:], ABS)
        sign = keep.tile([P, PACK], F32, name="sign")
        nc.scalar.activation(sign[:], gain[:], SIGN)
        picked_scales = gather_packed(d_scale_table[:], k1_t, U8, "picked_scales", "picked_scales")
        dealt_scales = keep.tile([P, PACK, P], U8, name="dealt_scales")
        nc.vector.tensor_copy(
            dealt_scales[:].rearrange("p t (c i) -> p c t i", i=16),
            picked_scales[:].rearrange("p (c i t) -> p c t i", i=16, t=PACK),
        )
        dealt_flat = dealt_scales[:].rearrange("p t m -> p (t m)").bitcast(I32)
        for i in range(4):
            source = 16 * (i // 2) + i % 2
            nc.sync.dma_start(d_scale_rows[i:P:32, :].bitcast(I32), dealt_flat[source:P:32, :])

        w1_codes, w1_scales = quantize(w1_bf[:].rearrange("p t m j -> p (t m j)"), H, "w1", "w1_codes")
        picked_words = gather_packed(d_table[:].bitcast(U32), k1_t, U32, "picked_words", "w1_bf")
        d_codes = keep.tile([P, H], U32, name="d_codes", align_bytes=64)
        nc.vector.tensor_copy(
            d_codes[:].rearrange("p (t c i) -> p c t i", i=4, t=PACK),
            picked_words[:].rearrange("p (c i t) -> p c t i", i=4, t=PACK),
        )

        y = []
        for t in range(PACK):
            if t == 2:
                cast_weight(w2_bf[:], w2_raw[:])
                w2_codes, w2_scales = quantize(w2_bf[:].rearrange("p t m j -> p (t m j)"), H, "w2", "w2_codes")
            acc = product(w1_codes, w1_scales, t, xa_words, xa_scales, S, t)
            y_t = keep.tile([P, S], F32, name="y%d" % t, tag="w2_raw" if t == 2 else "y%d" % t)
            nc.scalar.activation(y_t[:], acc[:], COPY, scale=size[:, t : t + 1])
            y.append(y_t)

        d = []
        for t in range(PACK):
            acc = product(w2_codes, w2_scales, t, xb_words, xb_scales, S, PACK + t)
            d_t = keep.tile([P, S], F32, name="d%d" % t)
            nc.scalar.activation(d_t[:], acc[:], COPY, scale=size[:, t : t + 1])
            d.append(d_t)

        sums = []
        for t in range(PACK):
            total = psum.tile([P, S], F32, name="total", tag="bank%d" % t)
            for b in range(BLOCKS):
                cols = slice(b * P, (b + 1) * P)
                nc.tensor.matmul(
                    total[:, cols], y[t][:, cols], ident_f32[:], start=(b == 0), stop=False, is_transpose=True
                )
            sums.append(total)
        lows = [psum.tile([P, PACK, CHUNK], BF16, name="back", tag="bank%d" % (PACK + c)) for c in range(CHUNKS)]
        for t in range(PACK):
            half = keep.tile([P, S], F32, name="half%d" % t)
            for c in range(CHUNKS):
                nc.vector.tensor_scalar(
                    half[:, c * CHUNK : (c + 1) * CHUNK],
                    y[t][:].indirect(n1_t[:, c * COLS : (c + 1) * COLS]),
                    -0.5,
                    0.0,
                    ALU.mult,
                    ALU.add,
                )
            for b in range(BLOCKS):
                cols = slice(b * P, (b + 1) * P)
                nc.tensor.matmul(
                    sums[t][:, cols], half[:, cols], ident_f32[:], start=False, stop=(b == BLOCKS - 1), is_transpose=True
                )
            turned = keep.tile([P, S], BF16, name="turned%d" % t)
            nc.scalar.copy(turned[:], sums[t][:])
            for b in range(BLOCKS):
                c, inner = divmod(b * P, CHUNK)
                nc.tensor.transpose(lows[c][:, t, inner : inner + P], turned[:, b * P : (b + 1) * P], ident_bf16[:])

        z_bf = []
        for c in range(CHUNKS):
            first = keep.tile([P, PACK, CHUNK], BF16, name="first%d" % c)
            nc.scalar.copy(first[:], lows[c][:])
            second = keep.tile([P, PACK, CHUNK], BF16, name="second%d" % c, tag="second")
            third = keep.tile([P, PACK, CHUNK], BF16, name="third%d" % c, tag="third")
            for t in range(PACK):
                nc.vector.tensor_copy(second[:, t, :], d[t][:].indirect(n2_t[:, c * COLS : (c + 1) * COLS]))
            least = keep.tile([P, PACK, CHUNK], BF16, name="least%d" % c, tag="woven%d" % (c - 1), align_bytes=64)
            for t in range(PACK):
                nc.vector.tensor_copy(third[:, t, :], d[t][:].indirect(n3_t[:, c * COLS : (c + 1) * COLS]))
                if t == 0:
                    nc.vector.tensor_tensor(least[:], first[:], second[:], ALU.min)
            clamp = keep.tile([P, PACK, CHUNK], BF16, name="clamp%d" % c)
            nc.vector.tensor_tensor(clamp[:], least[:], third[:], ALU.max)
            planes = keep.tile([P, PACK, CHUNK], BF16, name="planes%d" % c, tag="planes%d" % c)
            for t in range(PACK):
                nc.scalar.activation(planes[:, t, :], clamp[:, t, :], COPY, scale=sign[:, t : t + 1])
            woven = keep.tile([P, CHUNK, PACK], BF16, name="woven%d" % c, tag="woven%d" % c, align_bytes=64)
            nc.scalar.copy(
                woven[:].rearrange("p (c i) t -> p c t i", i=4), planes[:].rearrange("p t (c i) -> p c t i", i=4)
            )
            z_bf.append(quantize(woven[:].rearrange("p c t -> p (c t)"), CHUNK, "z%d" % c, "z_codes%d" % c))

        for c in range(CHUNKS):
            z_codes, z_scales = z_bf[c]
            for t in range(PACK):
                acc = product(d_codes, d_scale_rows, t, z_codes, z_scales, CHUNK, (c * 6 + t) % 8 if c == 0 or t < 2 else t + 2)
                h = keep.tile([P, CHUNK], F32, name="h%d_%d" % (c, t), tag="planes1" if (c, t) == (0, 2) else "h%d_%d" % (c, t))
                nc.scalar.activation(h[:], acc[:], COPY, scale=0.0625)
                nc.vector.tensor_copy(pages[t][:].indirect(n4_t[:, c * COLS : (c + 1) * COLS]), h[:])
                if c == CHUNKS - 1:
                    nc.sync.dma_start(out_rows[t], pages[t][:])
